import numpy as np
import ml_dtypes


def mxq(x, axis, fmt="e4m3"):
    dtype, down = {"e4m3": (ml_dtypes.float8_e4m3fn, 7), "e5m2": (ml_dtypes.float8_e5m2, 14)}[fmt]
    v = np.moveaxis(np.asarray(x, np.float32).astype(ml_dtypes.bfloat16).astype(np.float64), axis, -1)
    blocks = v.reshape(v.shape[:-1] + (-1, 32))
    amax = np.abs(blocks).max(-1, keepdims=True)
    byte = np.maximum(np.where(amax > 0, np.frexp(amax)[1] - 1 + 127, 0) - down, 1)
    scale = np.exp2(byte - 127.0)
    codes = (blocks / scale).astype(np.float32).astype(dtype).astype(np.float64)
    return np.moveaxis((codes * scale).reshape(v.shape), -1, axis)


WIDE = False


def mx_kscale(k):
    if not WIDE:
        return np.ones(k)
    levels = np.array([10, -10, 5, -5, 0])
    if k % 512:
        return np.exp2(np.random.permutation(np.resize(levels, k // 32))).repeat(32)
    a = np.empty((k // 512, 16))
    for p in range(k // 512):
        a[p, :8] = np.random.permutation(np.resize(levels, 8))
        for g in range(8):
            far = levels[np.abs(levels - a[p, g]) >= 10]
            a[p, g + 8] = far[np.random.randint(len(far))]
    return np.exp2(a.ravel()).repeat(32)


def f64(x):
    return np.asarray(x).astype(np.float64)


def striped(idx):
    return np.tile(idx.reshape(-1, 16).T, (8, 1)).astype(np.uint16)


def unstriped(offs):
    return offs[:16].T.reshape(-1).astype(np.int64)


def pack_weight(w):
    k, n = w.shape
    w = f64(np.asarray(w, np.float32).astype(ml_dtypes.bfloat16)).reshape(k // 32, 32, n)
    amax = np.abs(w).max(1)
    byte = np.clip(np.where(amax > 0, np.frexp(amax)[1] - 1 + 127 - 7, 1), 1, 254)
    scaled = (w * np.exp2(127.0 - byte)[:, None, :]).reshape(k, n).astype(np.float32)
    words = np.ascontiguousarray(scaled.reshape(k // 512, 128, 4, n).transpose(0, 1, 3, 2)).astype(ml_dtypes.float8_e4m3fn).view(np.uint8)
    return words, np.ascontiguousarray(byte.astype(np.uint8).reshape(k // 512, 16, n))


def unpack_weight(words, scales):
    g, p, n, _ = words.shape
    vals = np.ascontiguousarray(words).view(ml_dtypes.float8_e4m3fn).astype(np.float64) * np.repeat(np.exp2(scales.astype(np.float64) - 127.0), 8, axis=1)[..., None]
    return vals.transpose(0, 1, 3, 2).reshape(g * 512, n)


def planes(y):
    n, m = y.shape
    v = y.astype(np.float32).astype(ml_dtypes.bfloat16).astype(np.float64).reshape(n // 32, 32, m)
    top = np.abs(v).max(1)
    byte = np.clip(np.where(top > 0, np.frexp(top)[1] - 1 + 127 - 7, 1), 1, 254)
    codes = (v * np.exp2(127.0 - byte)[:, None, :]).reshape(n, m).astype(np.float32).astype(ml_dtypes.float8_e4m3fn).view(np.uint8)
    words = codes.reshape(n // 512, 128, 4, m).transpose(0, 1, 3, 2)
    return np.ascontiguousarray(words), np.ascontiguousarray(byte.astype(np.uint8).reshape(n // 512, 16, m))


K, T, S, N, H, W, U = 512, 2048, 512, 512, 512, 1024, 1024


def setup_inputs():
    n = np.random.standard_normal
    s = mx_kscale(K)[:, None]
    u = mx_kscale(H)
    packed_xT = pack_weight(n((K, T)) * s)
    packed_eT = pack_weight(n((K, W)) * s)
    return {
        "x_words": packed_xT[0],
        "x_scales": packed_xT[1],
        "w1": (n((K, N)) / np.sqrt(K) / s).astype(np.float32),
        "e_words": packed_eT[0],
        "e_scales": packed_eT[1],
        "w2": (n((K, N)) / np.sqrt(K) / s).astype(np.float32),
        "unit": (np.random.uniform(0.6, 1.4, (H, 1)) * u[:, None]).astype(np.float32),
        "w3": (n((H, N)) / np.sqrt(H) / u[:, None]).astype(np.float32),
        "offs": striped(np.random.permutation(T)[:S]),
        "ski": striped(np.random.permutation(W)[:S]),
        "ex": striped(np.random.permutation(np.concatenate([np.arange(S), np.random.randint(0, S, U - S)]))),
        "sk1": striped(np.random.permutation(np.concatenate([np.arange(S), np.random.randint(0, S, U - S)]))),
        "sk2": striped(np.random.permutation(np.concatenate([np.arange(S), np.random.randint(0, S, U - S)]))),
    }


def reference(x_words, x_scales, w1, e_words, e_scales, w2, unit, w3, offs, ski, ex, sk1, sk2):
    xq = unpack_weight(x_words, x_scales)[:, unstriped(offs)]
    y = mxq(f64(w1), 0, "e4m3").T @ xq
    y_1 = y[:, unstriped(ex)]
    e_ski = unpack_weight(e_words, e_scales)[:, unstriped(ski)]
    ye = mxq(f64(w2), 0, "e4m3").T @ e_ski
    e_1 = ye[:, unstriped(sk1)]
    mas = y_1 * e_1
    e_2 = ye[:, unstriped(sk2)]
    hid = f64(unit) * np.minimum(mas, e_2)
    out_0 = mxq(f64(w3), 0, "e4m3").T @ mxq(hid, 0, "e4m3")
    return (out_0,) + planes(out_0)

@@ -1,0 +1,223 @@
+from contextlib import ExitStack
+
+import concourse.mybir as mybir
+
+K, T, W, S, U = 512, 2048, 1024, 512, 1024
+P, PACK = 128, 4
+FLOPS = 2 * K * 512 * (S + S + U)
+
+F32 = mybir.dt.float32
+BF16 = mybir.dt.bfloat16
+I32 = mybir.dt.int32
+U32 = mybir.dt.uint32
+U16 = mybir.dt.uint16
+U8 = mybir.dt.uint8
+FP8X4 = mybir.dt.float8_e4m3fn_x4
+ALU = mybir.AluOpType
+ACT = mybir.ActivationFunctionType
+
+CHUNKS = (128, 256, 256, 256, 128)
+BANK = 512
+
+
+def tile_picked_ytutorq_min_po_kernel(
+    tc, x_words, x_scales, w1, e_words, e_scales, w2, unit, w3, offs, ski, ex, sk1, sk2, out_0, out_1, out_2
+):
+    nc = tc.nc
+    with ExitStack() as ctx:
+        keep = ctx.enter_context(tc.tile_pool(name="keep", bufs=1))
+        ring = ctx.enter_context(tc.tile_pool(name="ring", bufs=2))
+        psum = ctx.enter_context(tc.psum_pool(name="psum", bufs=8))
+
+        def load_list(name, src):
+            t = keep.tile([P, src.shape[1]], U16, name=name)
+            nc.sync.dma_start(t[:], src)
+            return t
+
+        def load_words(name, src):
+            t = keep.tile([P, src.shape[2]], I32, name=name)
+            nc.sync.dma_start(t[:], src[0].rearrange("p c r -> p (c r)").bitcast(I32))
+            return t
+
+        def cleared(name, src):
+            t = keep.tile([P, src.shape[2]], U8, name=name)
+            nc.gpsimd.memset(t[:].bitcast(I32), 0)
+            return t
+
+        def load_scales(t, src):
+            for q in range(4):
+                nc.sync.dma_start(t[32 * q : 32 * q + 4, :].bitcast(I32), src[0, 4 * q : 4 * q + 4, :].bitcast(I32))
+
+        def load_weight(name, src, parts):
+            cols = 512 // parts
+            tiles = []
+            for h in range(parts):
+                t = ring.tile([P, PACK, cols], F32, name="w_raw", bufs=4)
+                nc.sync.dma_start(t[:], src[:, h * cols : (h + 1) * cols].rearrange("(p j) c -> p j c", j=PACK))
+                tiles.append(t)
+            return tiles
+
+        def dealt(grouped, h, parts):
+            m = P // parts
+            return grouped[:, :, h * m : (h + 1) * m, :].rearrange("p t m j -> p m j t")
+
+        def as_loaded(raw):
+            return raw[:].rearrange("p j (m t) -> p m j t", t=PACK)
+
+        def quantize_weight(name, grouped, calls):
+            codes = keep.tile([P, 512], U32, name=name + "_codes", align_bytes=64)
+            scales = keep.tile([P, 512], U8, name=name + "_scales", align_bytes=64)
+            flat = grouped[:].rearrange("p t m j -> p (t m j)")
+            n = 512 // calls
+            for c in range(calls):
+                nc.vector.quantize_mx(
+                    out=codes[:, c * n : (c + 1) * n].bitcast(FP8X4),
+                    scales=scales[:, c * n : (c + 1) * n],
+                    in_=flat[:, PACK * c * n : PACK * (c + 1) * n],
+                )
+            return codes, scales
+
+        def pick(name, table, offsets, dtype):
+            t = keep.tile([P, S], dtype, name=name, align_bytes=64)
+            nc.vector.tensor_copy(t[:], table.indirect(offsets[:]))
+            return t
+
+        def product(out, weight, t, codes, scales):
+            nc.tensor.matmul_mx(
+                out=out,
+                lhsT=weight[0][:, t * P : (t + 1) * P].bitcast(FP8X4),
+                lhsT_scale=weight[1][:, t * P : (t + 1) * P],
+                rhs=codes.bitcast(FP8X4),
+                rhs_scale=scales,
+                start=True,
+                stop=True,
+            )
+
+        es = cleared("es", e_scales)
+        xs = cleared("xs", x_scales)
+        ski_t = load_list("ski_t", ski)
+        ew = load_words("ew", e_words)
+        load_scales(es, e_scales)
+        w2_raw = load_weight("w_raw", w2, 2)
+        unit_t = keep.tile([P, PACK], F32, name="unit_t")
+        nc.sync.dma_start(unit_t[:], unit.rearrange("(p t) o -> p (t o)", t=PACK))
+        sk1_t = load_list("sk1_t", sk1)
+        sk2_t = load_list("sk2_t", sk2)
+        offs_t = load_list("offs_t", offs)
+        load_scales(xs, x_scales)
+        xw = load_words("xw", x_words)
+        ex_t = load_list("ex_t", ex)
+
+        size = keep.tile([P, PACK], F32, name="size")
+        nc.scalar.activation(size[:], unit_t[:], ACT.Abs)
+        positive = keep.tile([P, PACK], F32, name="positive")
+        nc.gpsimd.tensor_scalar(positive[:], unit_t[:], 0.0, 2.0, ALU.is_ge, ALU.mult)
+        sign_t = keep.tile([P, PACK], F32, name="sign_t")
+        nc.gpsimd.tensor_scalar(sign_t[:], positive[:], 1.0, -1.0, ALU.mult, ALU.add)
+
+        e_codes = pick("e_codes", ew[:].bitcast(U32), ski_t, U32)
+        e_bytes = pick("e_bytes", es[:], ski_t, U8)
+        w2_g = keep.tile([P, PACK, P, PACK], BF16, name="w2_g", align_bytes=64)
+        nc.scalar.copy(dealt(w2_g, 0, 2), as_loaded(w2_raw[0]))
+        nc.vector.tensor_copy(dealt(w2_g, 1, 2), as_loaded(w2_raw[1]))
+        w2_q = quantize_weight("w2", w2_g, 4)
+        ye = []
+        for t in range(PACK):
+            bank = psum.tile([P, BANK], F32, name="bank")
+            product(bank[:], w2_q, t, e_codes[:], e_bytes[:])
+            row = keep.tile([P, S], F32, name="ye" + str(t))
+            nc.scalar.activation(row[:], bank[:], ACT.Copy, scale=size[:, t : t + 1])
+            ye.append(row)
+
+        w1_raw = load_weight("w_raw", w1, 2)
+        x_bytes = pick("x_bytes", xs[:], offs_t, U8)
+        x_codes = pick("x_codes", xw[:].bitcast(U32), offs_t, U32)
+        w1_g = keep.tile([P, PACK, P, PACK], BF16, name="w1_g", align_bytes=64)
+        for h in range(2):
+            nc.vector.tensor_copy(dealt(w1_g, h, 2), as_loaded(w1_raw[h]))
+        w1_q = quantize_weight("w1", w1_g, 4)
+        y = []
+        for t in range(PACK):
+            bank = psum.tile([P, BANK], F32, name="bank")
+            product(bank[:], w1_q, t, x_codes[:], x_bytes[:])
+            row = keep.tile([P, S], F32, name="y" + str(t))
+            if t < 2:
+                nc.vector.tensor_copy(row[:], bank[:])
+            else:
+                nc.scalar.copy(row[:], bank[:])
+            y.append(row)
+
+        w3_raw = load_weight("w3_raw", w3, 2)
+        w3_g = keep.tile([P, PACK, P, PACK], BF16, name="w3_g", align_bytes=64)
+        for h in range(2):
+            nc.vector.tensor_tensor(
+                dealt(w3_g, h, 2),
+                as_loaded(w3_raw[h]),
+                sign_t[:].unsqueeze(1).unsqueeze(3).to_broadcast([P, P // 2, PACK, PACK]),
+                ALU.mult,
+            )
+        w3_q = quantize_weight("w3", w3_g, 1)
+
+        out_codes = keep.tile([P, U], U32, name="out_codes", align_bytes=64)
+        out_scales = keep.tile([P, U], U8, name="out_scales", align_bytes=64)
+        out_rows = out_0.rearrange("(p t) r -> p t r", t=PACK)
+        out_words = out_1[0].rearrange("p c r -> p (c r)").bitcast(I32)
+        widest = max(CHUNKS)
+
+        def woven(tile, n):
+            return tile[:, :n, :].rearrange("p (c i) t -> p c t i", i=4)
+
+        def by_rows(tile, n):
+            return tile[:, : PACK * n].rearrange("p (t c i) -> p c t i", t=PACK, i=4)
+
+        def hidden(r0, n):
+            cols = slice(r0 // 16, (r0 + n) // 16)
+            mas = ring.tile([P, PACK * widest], F32, name="mas")
+            e_2 = ring.tile([P, PACK * widest], F32, name="e_2")
+            for t in range(PACK):
+                e_1 = ring.tile([P, widest], F32, name="e_1", bufs=4)
+                nc.scalar.activation(e_1[:, :n], ye[t][:].indirect(sk1_t[:, cols]), ACT.Copy)
+                nc.vector.tensor_tensor(mas[:, t * n : (t + 1) * n], y[t][:].indirect(ex_t[:, cols]), e_1[:, :n], ALU.mult)
+            for t in range(PACK):
+                nc.scalar.activation(e_2[:, t * n : (t + 1) * n], ye[t][:].indirect(sk2_t[:, cols]), ACT.Copy)
+            hid = ring.tile([P, widest, PACK], BF16, name="hid", align_bytes=64)
+            nc.vector.tensor_tensor(woven(hid, n), by_rows(mas, n), by_rows(e_2, n), ALU.min)
+            codes = ring.tile([P, widest], U32, name="hid_codes", align_bytes=64)
+            scales = ring.tile([P, widest], U8, name="hid_scales", align_bytes=64)
+            nc.vector.quantize_mx(
+                out=codes[:, :n].bitcast(FP8X4), scales=scales[:, :n], in_=hid[:, :n, :].rearrange("p c t -> p (c t)")
+            )
+            banks = []
+            per_bank = BANK // n
+            for t in range(PACK):
+                if t % per_bank == 0:
+                    banks.append(psum.tile([P, BANK], F32, name="bank"))
+                product(banks[-1][:, (t % per_bank) * n : (t % per_bank + 1) * n], w3_q, t, codes[:, :n], scales[:, :n])
+            return banks
+
+        def hand_out(r0, n, banks):
+            res = ring.tile([P, PACK * widest], F32, name="res")
+            for b, bank in enumerate(banks):
+                nc.scalar.copy(res[:, b * BANK : (b + 1) * BANK], bank[:])
+            nc.sync.dma_start(out_rows[:, :, r0 : r0 + n], res[:, : PACK * n].rearrange("p (t c) -> p t c", t=PACK))
+            rounded = ring.tile([P, widest, PACK], BF16, name="rounded", align_bytes=64)
+            nc.vector.tensor_copy(woven(rounded, n), by_rows(res, n))
+            nc.vector.quantize_mx(
+                out=out_codes[:, r0 : r0 + n].bitcast(FP8X4),
+                scales=out_scales[:, r0 : r0 + n],
+                in_=rounded[:, :n, :].rearrange("p c t -> p (c t)"),
+            )
+            nc.sync.dma_start(out_words[:, r0 : r0 + n], out_codes[:, r0 : r0 + n].bitcast(I32))
+
+        pending = None
+        r0 = 0
+        for n in CHUNKS:
+            banks = hidden(r0, n)
+            if pending is not None:
+                hand_out(*pending)
+            pending = (r0, n, banks)
+            r0 = r0 + n
+        hand_out(*pending)
+        for q in range(4):
+            queue = nc.scalar if q % 2 else nc.sync
+            queue.dma_start(out_2[0, 4 * q : 4 * q + 4, :].bitcast(I32), out_scales[32 * q : 32 * q + 4, :].bitcast(I32))

@@ -16,7 +16,21 @@ FP8X4 = mybir.dt.float8_e4m3fn_x4
 ALU = mybir.AluOpType
 ACT = mybir.ActivationFunctionType
 
-CHUNKS = (128, 256, 256, 256, 128)
+CHUNKS = (384, 256, 256, 128)
+E1B = 4
+E2MODE = 5
+YV = 1
+V2 = 1
+XFIRST = 1
+W3LATE = 0
+MASB = 2
+RESB = 2
+V2L = 0
+HEAD = 0
+Q1 = 1
+Q2 = 4
+SPLIT = 2
+SPARE = 0
 BANK = 512
 
 
@@ -44,9 +58,9 @@ def tile_picked_ytutorq_min_po_kernel(
             nc.gpsimd.memset(t[:].bitcast(I32), 0)
             return t
 
-        def load_scales(t, src):
+        def load_scales(queue, t, src):
             for q in range(4):
-                nc.sync.dma_start(t[32 * q : 32 * q + 4, :].bitcast(I32), src[0, 4 * q : 4 * q + 4, :].bitcast(I32))
+                queue.dma_start(t[32 * q : 32 * q + 4, :].bitcast(I32), src[0, 4 * q : 4 * q + 4, :].bitcast(I32))
 
         def load_weight(name, src, parts):
             cols = 512 // parts
@@ -96,16 +110,28 @@ def tile_picked_ytutorq_min_po_kernel(
         es = cleared("es", e_scales)
         xs = cleared("xs", x_scales)
         ski_t = load_list("ski_t", ski)
-        ew = load_words("ew", e_words)
-        load_scales(es, e_scales)
-        w2_raw = load_weight("w_raw", w2, 2)
+        if HEAD == 0:
+            ew = load_words("ew", e_words)
+            load_scales(nc.sync, es, e_scales)
+            w2_raw = load_weight("w_raw", w2, 2)
+        else:
+            load_scales(nc.sync, es, e_scales)
+            w2_raw = load_weight("w_raw", w2, 2)
+            ew = load_words("ew", e_words)
         unit_t = keep.tile([P, PACK], F32, name="unit_t")
         nc.sync.dma_start(unit_t[:], unit.rearrange("(p t) o -> p (t o)", t=PACK))
         sk1_t = load_list("sk1_t", sk1)
         sk2_t = load_list("sk2_t", sk2)
-        offs_t = load_list("offs_t", offs)
-        load_scales(xs, x_scales)
-        xw = load_words("xw", x_words)
+        if XFIRST:
+            xw = load_words("xw", x_words)
+            offs_t = load_list("offs_t", offs)
+            load_scales(nc.sync, xs, x_scales)
+            w1_raw = load_weight("w_raw", w1, 2)
+        else:
+            w1_raw = load_weight("w_raw", w1, 2)
+            offs_t = load_list("offs_t", offs)
+            load_scales(nc.sync, xs, x_scales)
+            xw = load_words("xw", x_words)
         ex_t = load_list("ex_t", ex)
 
         size = keep.tile([P, PACK], F32, name="size")
@@ -115,12 +141,16 @@ def tile_picked_ytutorq_min_po_kernel(
         sign_t = keep.tile([P, PACK], F32, name="sign_t")
         nc.gpsimd.tensor_scalar(sign_t[:], positive[:], 1.0, -1.0, ALU.mult, ALU.add)
 
+        e_bytes = pick("e_bytes", es[:], ski_t, U8) if HEAD else None
         e_codes = pick("e_codes", ew[:].bitcast(U32), ski_t, U32)
-        e_bytes = pick("e_bytes", es[:], ski_t, U8)
+        e_bytes = e_bytes if HEAD else pick("e_bytes", es[:], ski_t, U8)
         w2_g = keep.tile([P, PACK, P, PACK], BF16, name="w2_g", align_bytes=64)
         nc.scalar.copy(dealt(w2_g, 0, 2), as_loaded(w2_raw[0]))
-        nc.vector.tensor_copy(dealt(w2_g, 1, 2), as_loaded(w2_raw[1]))
-        w2_q = quantize_weight("w2", w2_g, 4)
+        if HEAD:
+            nc.scalar.copy(dealt(w2_g, 1, 2), as_loaded(w2_raw[1]))
+        else:
+            nc.vector.tensor_copy(dealt(w2_g, 1, 2), as_loaded(w2_raw[1]))
+        w2_q = quantize_weight("w2", w2_g, Q2)
         ye = []
         for t in range(PACK):
             bank = psum.tile([P, BANK], F32, name="bank")
@@ -129,34 +159,39 @@ def tile_picked_ytutorq_min_po_kernel(
             nc.scalar.activation(row[:], bank[:], ACT.Copy, scale=size[:, t : t + 1])
             ye.append(row)
 
-        w1_raw = load_weight("w_raw", w1, 2)
-        x_bytes = pick("x_bytes", xs[:], offs_t, U8)
-        x_codes = pick("x_codes", xw[:].bitcast(U32), offs_t, U32)
-        w1_g = keep.tile([P, PACK, P, PACK], BF16, name="w1_g", align_bytes=64)
+        w1_g = keep.tile([P, PACK, P, PACK], BF16, name="w1_g", tag="stage0", align_bytes=64)
         for h in range(2):
             nc.vector.tensor_copy(dealt(w1_g, h, 2), as_loaded(w1_raw[h]))
-        w1_q = quantize_weight("w1", w1_g, 4)
+        w1_q = quantize_weight("w1", w1_g, Q1)
+        x_bytes = pick("x_bytes", xs[:], offs_t, U8)
+        x_codes = pick("x_codes", xw[:].bitcast(U32), offs_t, U32)
         y = []
         for t in range(PACK):
             bank = psum.tile([P, BANK], F32, name="bank")
             product(bank[:], w1_q, t, x_codes[:], x_bytes[:])
             row = keep.tile([P, S], F32, name="y" + str(t))
-            if t < 2:
+            if t < YV:
                 nc.vector.tensor_copy(row[:], bank[:])
             else:
                 nc.scalar.copy(row[:], bank[:])
             y.append(row)
 
         w3_raw = load_weight("w3_raw", w3, 2)
-        w3_g = keep.tile([P, PACK, P, PACK], BF16, name="w3_g", align_bytes=64)
-        for h in range(2):
-            nc.vector.tensor_tensor(
-                dealt(w3_g, h, 2),
-                as_loaded(w3_raw[h]),
-                sign_t[:].unsqueeze(1).unsqueeze(3).to_broadcast([P, P // 2, PACK, PACK]),
-                ALU.mult,
-            )
-        w3_q = quantize_weight("w3", w3_g, 1)
+        w3_g = keep.tile([P, PACK, P, PACK], BF16, name="w3_g", tag="stage1", align_bytes=64)
+        w3_box = []
+
+        def make_w3():
+            for h in range(2):
+                nc.vector.tensor_tensor(
+                    dealt(w3_g, h, 2),
+                    as_loaded(w3_raw[h]),
+                    sign_t[:].unsqueeze(1).unsqueeze(3).to_broadcast([P, P // 2, PACK, PACK]),
+                    ALU.mult,
+                )
+            w3_box.append(quantize_weight("w3", w3_g, 1))
+
+        if not W3LATE:
+            make_w3()
 
         out_codes = keep.tile([P, U], U32, name="out_codes", align_bytes=64)
         out_scales = keep.tile([P, U], U8, name="out_scales", align_bytes=64)
@@ -170,16 +205,28 @@ def tile_picked_ytutorq_min_po_kernel(
         def by_rows(tile, n):
             return tile[:, : PACK * n].rearrange("p (t c i) -> p c t i", t=PACK, i=4)
 
-        def hidden(r0, n):
+        def hidden(c, r0, n):
             cols = slice(r0 // 16, (r0 + n) // 16)
-            mas = ring.tile([P, PACK * widest], F32, name="mas")
-            e_2 = ring.tile([P, PACK * widest], F32, name="e_2")
+            mas = ring.tile([P, PACK * widest], F32, name="mas", bufs=MASB)
+            if E2MODE == 0:
+                e_2 = keep.tile([P, PACK * widest], F32, name="e_2", tag="stage" + str(c % 2), align_bytes=64)
+            elif E2MODE == 1:
+                e_2 = keep.tile([P, PACK * widest], F32, name="e_2", tag="stage0" if c % 2 else "free", align_bytes=64)
+            elif E2MODE == 4:
+                e_2 = keep.tile([P, PACK * widest], F32, name="e_2", tag="w1_codes" if c % 2 else "free", align_bytes=64)
+            elif E2MODE == 5:
+                e_2 = keep.tile([P, PACK * widest], F32, name="e_2", tag="w1_codes" if c % 2 else "stage0", align_bytes=64)
+            else:
+                e_2 = ring.tile([P, PACK * widest], F32, name="e_2", bufs=E2MODE)
             for t in range(PACK):
-                e_1 = ring.tile([P, widest], F32, name="e_1", bufs=4)
+                e_1 = ring.tile([P, widest], F32, name="e_1", bufs=E1B)
                 nc.scalar.activation(e_1[:, :n], ye[t][:].indirect(sk1_t[:, cols]), ACT.Copy)
                 nc.vector.tensor_tensor(mas[:, t * n : (t + 1) * n], y[t][:].indirect(ex_t[:, cols]), e_1[:, :n], ALU.mult)
             for t in range(PACK):
-                nc.scalar.activation(e_2[:, t * n : (t + 1) * n], ye[t][:].indirect(sk2_t[:, cols]), ACT.Copy)
+                if c * PACK + t < V2 or (c == len(CHUNKS) - 1 and t >= PACK - V2L):
+                    nc.vector.tensor_copy(e_2[:, t * n : (t + 1) * n], ye[t][:].indirect(sk2_t[:, cols]))
+                else:
+                    nc.scalar.activation(e_2[:, t * n : (t + 1) * n], ye[t][:].indirect(sk2_t[:, cols]), ACT.Copy)
             hid = ring.tile([P, widest, PACK], BF16, name="hid", align_bytes=64)
             nc.vector.tensor_tensor(woven(hid, n), by_rows(mas, n), by_rows(e_2, n), ALU.min)
             codes = ring.tile([P, widest], U32, name="hid_codes", align_bytes=64)
@@ -187,18 +234,28 @@ def tile_picked_ytutorq_min_po_kernel(
             nc.vector.quantize_mx(
                 out=codes[:, :n].bitcast(FP8X4), scales=scales[:, :n], in_=hid[:, :n, :].rearrange("p c t -> p (c t)")
             )
-            banks = []
-            per_bank = BANK // n
+            if not w3_box:
+                make_w3()
+            w3_q = w3_box[0]
+            fill = PACK * n // 2 if (SPLIT and c == len(CHUNKS) - 1) else min(BANK, PACK * n)
+            banks = [psum.tile([P, BANK], F32, name="bank") for b in range(PACK * n // fill)]
             for t in range(PACK):
-                if t % per_bank == 0:
-                    banks.append(psum.tile([P, BANK], F32, name="bank"))
-                product(banks[-1][:, (t % per_bank) * n : (t % per_bank + 1) * n], w3_q, t, codes[:, :n], scales[:, :n])
+                lo = 0
+                while lo < n:
+                    b, at = divmod(t * n + lo, fill)
+                    width = 512 if n == 512 else 256 if min(n - lo, fill - at) >= 256 else min(n, 128)
+                    product(banks[b][:, at : at + width], w3_q, t, codes[:, lo : lo + width], scales[:, lo : lo + width])
+                    lo = lo + width
             return banks
 
         def hand_out(r0, n, banks):
-            res = ring.tile([P, PACK * widest], F32, name="res")
+            res = ring.tile([P, PACK * widest], F32, name="res", bufs=RESB)
             for b, bank in enumerate(banks):
-                nc.scalar.copy(res[:, b * BANK : (b + 1) * BANK], bank[:])
+                used = PACK * n // len(banks)
+                if SPLIT == 2 and r0 + n == U and b == 1:
+                    nc.vector.tensor_copy(res[:, b * used : (b + 1) * used], bank[:, :used])
+                else:
+                    nc.scalar.copy(res[:, b * used : (b + 1) * used], bank[:, :used])
             nc.sync.dma_start(out_rows[:, :, r0 : r0 + n], res[:, : PACK * n].rearrange("p (t c) -> p t c", t=PACK))
             rounded = ring.tile([P, widest, PACK], BF16, name="rounded", align_bytes=64)
             nc.vector.tensor_copy(woven(rounded, n), by_rows(res, n))
@@ -211,8 +268,8 @@ def tile_picked_ytutorq_min_po_kernel(
 
         pending = None
         r0 = 0
-        for n in CHUNKS:
-            banks = hidden(r0, n)
+        for c, n in enumerate(CHUNKS):
+            banks = hidden(c, r0, n)
             if pending is not None:
                 hand_out(*pending)
             pending = (r0, n, banks)

@@ -71,12 +71,23 @@ def tile_picked_ytutorq_min_po_kernel(
                 tiles.append(t)
             return tiles
 
+        def load_half(src, h):
+            t = ring.tile([P, PACK, 256], F32, name="w_raw", bufs=4)
+            nc.sync.dma_start(t[:], src[:, h * 256 : (h + 1) * 256].rearrange("(p j) c -> p j c", j=PACK))
+            return t
+
         def dealt(grouped, h, parts):
             m = P // parts
             return grouped[:, :, h * m : (h + 1) * m, :].rearrange("p t m j -> p m j t")
 
         def as_loaded(raw):
             return raw[:].rearrange("p j (m t) -> p m j t", t=PACK)
+
+        def deal(grouped, raw, h, copy=nc.vector.tensor_copy):
+            copy(
+                grouped[:, :, 64 * h : 64 * h + 64, :].rearrange("p (u v) m j -> p u m j v", v=2),
+                raw[:].rearrange("p j (m u v) -> p u m j v", u=2, v=2),
+            )
 
         def quantize_weight(name, grouped, calls):
             codes = keep.tile([P, 512], U32, name=name + "_codes", align_bytes=64)
@@ -111,9 +122,10 @@ def tile_picked_ytutorq_min_po_kernel(
         xs = cleared("xs", x_scales)
         ski_t = load_list("ski_t", ski)
         if HEAD == 0:
-            ew = load_words("ew", e_words)
+            w2_raw = [load_half(w2, 0)]
             load_scales(nc.sync, es, e_scales)
-            w2_raw = load_weight("w_raw", w2, 2)
+            ew = load_words("ew", e_words)
+            w2_raw.append(load_half(w2, 1))
         else:
             load_scales(nc.sync, es, e_scales)
             w2_raw = load_weight("w_raw", w2, 2)
@@ -141,15 +153,11 @@ def tile_picked_ytutorq_min_po_kernel(
         sign_t = keep.tile([P, PACK], F32, name="sign_t")
         nc.gpsimd.tensor_scalar(sign_t[:], positive[:], 1.0, -1.0, ALU.mult, ALU.add)
 
-        e_bytes = pick("e_bytes", es[:], ski_t, U8) if HEAD else None
-        e_codes = pick("e_codes", ew[:].bitcast(U32), ski_t, U32)
-        e_bytes = e_bytes if HEAD else pick("e_bytes", es[:], ski_t, U8)
         w2_g = keep.tile([P, PACK, P, PACK], BF16, name="w2_g", align_bytes=64)
-        nc.scalar.copy(dealt(w2_g, 0, 2), as_loaded(w2_raw[0]))
-        if HEAD:
-            nc.scalar.copy(dealt(w2_g, 1, 2), as_loaded(w2_raw[1]))
-        else:
-            nc.vector.tensor_copy(dealt(w2_g, 1, 2), as_loaded(w2_raw[1]))
+        deal(w2_g, w2_raw[0], 0, nc.scalar.copy)
+        e_bytes = pick("e_bytes", es[:], ski_t, U8)
+        e_codes = pick("e_codes", ew[:].bitcast(U32), ski_t, U32)
+        deal(w2_g, w2_raw[1], 1)
         w2_q = quantize_weight("w2", w2_g, Q2)
         ye = []
         for t in range(PACK):
@@ -161,7 +169,7 @@ def tile_picked_ytutorq_min_po_kernel(
 
         w1_g = keep.tile([P, PACK, P, PACK], BF16, name="w1_g", tag="stage0", align_bytes=64)
         for h in range(2):
-            nc.vector.tensor_copy(dealt(w1_g, h, 2), as_loaded(w1_raw[h]))
+            deal(w1_g, w1_raw[h], h)
         w1_q = quantize_weight("w1", w1_g, Q1)
         x_bytes = pick("x_bytes", xs[:], offs_t, U8)
         x_codes = pick("x_codes", xw[:].bitcast(U32), offs_t, U32)

from contextlib import ExitStack

import concourse.mybir as mybir

K, T, W, S, U = 512, 2048, 1024, 512, 1024
P, PACK = 128, 4
FLOPS = 2 * K * 512 * (S + S + U)

F32 = mybir.dt.float32
BF16 = mybir.dt.bfloat16
I32 = mybir.dt.int32
U32 = mybir.dt.uint32
U16 = mybir.dt.uint16
U8 = mybir.dt.uint8
FP8X4 = mybir.dt.float8_e4m3fn_x4
ALU = mybir.AluOpType
ACT = mybir.ActivationFunctionType

CHUNKS = (384, 256, 256, 128)
E1B = 4
E2MODE = 5
YV = 1
V2 = 1
XFIRST = 1
W3LATE = 0
MASB = 2
RESB = 2
V2L = 0
HEAD = 0
Q1 = 1
Q2 = 4
SPLIT = 2
SPARE = 0
BANK = 512


def tile_picked_ytutorq_min_po_kernel(
    tc, x_words, x_scales, w1, e_words, e_scales, w2, unit, w3, offs, ski, ex, sk1, sk2, out_0, out_1, out_2
):
    nc = tc.nc
    with ExitStack() as ctx:
        keep = ctx.enter_context(tc.tile_pool(name="keep", bufs=1))
        ring = ctx.enter_context(tc.tile_pool(name="ring", bufs=2))
        psum = ctx.enter_context(tc.psum_pool(name="psum", bufs=8))

        def load_list(name, src):
            t = keep.tile([P, src.shape[1]], U16, name=name)
            nc.sync.dma_start(t[:], src)
            return t

        def load_words(name, src):
            t = keep.tile([P, src.shape[2]], I32, name=name)
            nc.sync.dma_start(t[:], src[0].rearrange("p c r -> p (c r)").bitcast(I32))
            return t

        def cleared(name, src):
            t = keep.tile([P, src.shape[2]], U8, name=name)
            nc.gpsimd.memset(t[:].bitcast(I32), 0)
            return t

        def load_scales(queue, t, src):
            for q in range(4):
                queue.dma_start(t[32 * q : 32 * q + 4, :].bitcast(I32), src[0, 4 * q : 4 * q + 4, :].bitcast(I32))

        def load_weight(name, src, parts):
            cols = 512 // parts
            tiles = []
            for h in range(parts):
                t = ring.tile([P, PACK, cols], F32, name="w_raw", bufs=4)
                nc.sync.dma_start(t[:], src[:, h * cols : (h + 1) * cols].rearrange("(p j) c -> p j c", j=PACK))
                tiles.append(t)
            return tiles

        def load_half(src, h):
            t = ring.tile([P, PACK, 256], F32, name="w_raw", bufs=4)
            nc.sync.dma_start(t[:], src[:, h * 256 : (h + 1) * 256].rearrange("(p j) c -> p j c", j=PACK))
            return t

        def dealt(grouped, h, parts):
            m = P // parts
            return grouped[:, :, h * m : (h + 1) * m, :].rearrange("p t m j -> p m j t")

        def as_loaded(raw):
            return raw[:].rearrange("p j (m t) -> p m j t", t=PACK)

        def deal(grouped, raw, h, copy=nc.vector.tensor_copy):
            copy(
                grouped[:, :, 64 * h : 64 * h + 64, :].rearrange("p (u v) m j -> p u m j v", v=2),
                raw[:].rearrange("p j (m u v) -> p u m j v", u=2, v=2),
            )

        def quantize_weight(name, grouped, calls):
            codes = keep.tile([P, 512], U32, name=name + "_codes", align_bytes=64)
            scales = keep.tile([P, 512], U8, name=name + "_scales", align_bytes=64)
            flat = grouped[:].rearrange("p t m j -> p (t m j)")
            n = 512 // calls
            for c in range(calls):
                nc.vector.quantize_mx(
                    out=codes[:, c * n : (c + 1) * n].bitcast(FP8X4),
                    scales=scales[:, c * n : (c + 1) * n],
                    in_=flat[:, PACK * c * n : PACK * (c + 1) * n],
                )
            return codes, scales

        def pick(name, table, offsets, dtype):
            t = keep.tile([P, S], dtype, name=name, align_bytes=64)
            nc.vector.tensor_copy(t[:], table.indirect(offsets[:]))
            return t

        def product(out, weight, t, codes, scales):
            nc.tensor.matmul_mx(
                out=out,
                lhsT=weight[0][:, t * P : (t + 1) * P].bitcast(FP8X4),
                lhsT_scale=weight[1][:, t * P : (t + 1) * P],
                rhs=codes.bitcast(FP8X4),
                rhs_scale=scales,
                start=True,
                stop=True,
            )

        es = cleared("es", e_scales)
        xs = cleared("xs", x_scales)
        ski_t = load_list("ski_t", ski)
        if HEAD == 0:
            w2_raw = [load_half(w2, 0)]
            load_scales(nc.sync, es, e_scales)
            ew = load_words("ew", e_words)
            w2_raw.append(load_half(w2, 1))
        else:
            load_scales(nc.sync, es, e_scales)
            w2_raw = load_weight("w_raw", w2, 2)
            ew = load_words("ew", e_words)
        unit_t = keep.tile([P, PACK], F32, name="unit_t")
        nc.sync.dma_start(unit_t[:], unit.rearrange("(p t) o -> p (t o)", t=PACK))
        sk1_t = load_list("sk1_t", sk1)
        sk2_t = load_list("sk2_t", sk2)
        if XFIRST:
            xw = load_words("xw", x_words)
            offs_t = load_list("offs_t", offs)
            load_scales(nc.sync, xs, x_scales)
            w1_raw = load_weight("w_raw", w1, 2)
        else:
            w1_raw = load_weight("w_raw", w1, 2)
            offs_t = load_list("offs_t", offs)
            load_scales(nc.sync, xs, x_scales)
            xw = load_words("xw", x_words)
        ex_t = load_list("ex_t", ex)

        size = keep.tile([P, PACK], F32, name="size")
        nc.scalar.activation(size[:], unit_t[:], ACT.Abs)
        positive = keep.tile([P, PACK], F32, name="positive")
        nc.gpsimd.tensor_scalar(positive[:], unit_t[:], 0.0, 2.0, ALU.is_ge, ALU.mult)
        sign_t = keep.tile([P, PACK], F32, name="sign_t")
        nc.gpsimd.tensor_scalar(sign_t[:], positive[:], 1.0, -1.0, ALU.mult, ALU.add)

        w2_g = keep.tile([P, PACK, P, PACK], BF16, name="w2_g", align_bytes=64)
        deal(w2_g, w2_raw[0], 0, nc.scalar.copy)
        e_bytes = pick("e_bytes", es[:], ski_t, U8)
        e_codes = pick("e_codes", ew[:].bitcast(U32), ski_t, U32)
        deal(w2_g, w2_raw[1], 1)
        w2_q = quantize_weight("w2", w2_g, Q2)
        ye = []
        for t in range(PACK):
            bank = psum.tile([P, BANK], F32, name="bank")
            product(bank[:], w2_q, t, e_codes[:], e_bytes[:])
            row = keep.tile([P, S], F32, name="ye" + str(t))
            nc.scalar.activation(row[:], bank[:], ACT.Copy, scale=size[:, t : t + 1])
            ye.append(row)

        w1_g = keep.tile([P, PACK, P, PACK], BF16, name="w1_g", tag="stage0", align_bytes=64)
        for h in range(2):
            deal(w1_g, w1_raw[h], h)
        w1_q = quantize_weight("w1", w1_g, Q1)
        x_bytes = pick("x_bytes", xs[:], offs_t, U8)
        x_codes = pick("x_codes", xw[:].bitcast(U32), offs_t, U32)
        y = []
        for t in range(PACK):
            bank = psum.tile([P, BANK], F32, name="bank")
            product(bank[:], w1_q, t, x_codes[:], x_bytes[:])
            row = keep.tile([P, S], F32, name="y" + str(t))
            if t < YV:
                nc.vector.tensor_copy(row[:], bank[:])
            else:
                nc.scalar.copy(row[:], bank[:])
            y.append(row)

        w3_raw = load_weight("w3_raw", w3, 2)
        w3_g = keep.tile([P, PACK, P, PACK], BF16, name="w3_g", tag="stage1", align_bytes=64)
        w3_box = []

        def make_w3():
            for h in range(2):
                nc.vector.tensor_tensor(
                    dealt(w3_g, h, 2),
                    as_loaded(w3_raw[h]),
                    sign_t[:].unsqueeze(1).unsqueeze(3).to_broadcast([P, P // 2, PACK, PACK]),
                    ALU.mult,
                )
            w3_box.append(quantize_weight("w3", w3_g, 1))

        if not W3LATE:
            make_w3()

        out_codes = keep.tile([P, U], U32, name="out_codes", align_bytes=64)
        out_scales = keep.tile([P, U], U8, name="out_scales", align_bytes=64)
        out_rows = out_0.rearrange("(p t) r -> p t r", t=PACK)
        out_words = out_1[0].rearrange("p c r -> p (c r)").bitcast(I32)
        widest = max(CHUNKS)

        def woven(tile, n):
            return tile[:, :n, :].rearrange("p (c i) t -> p c t i", i=4)

        def by_rows(tile, n):
            return tile[:, : PACK * n].rearrange("p (t c i) -> p c t i", t=PACK, i=4)

        def hidden(c, r0, n):
            cols = slice(r0 // 16, (r0 + n) // 16)
            mas = ring.tile([P, PACK * widest], F32, name="mas", bufs=MASB)
            if E2MODE == 0:
                e_2 = keep.tile([P, PACK * widest], F32, name="e_2", tag="stage" + str(c % 2), align_bytes=64)
            elif E2MODE == 1:
                e_2 = keep.tile([P, PACK * widest], F32, name="e_2", tag="stage0" if c % 2 else "free", align_bytes=64)
            elif E2MODE == 4:
                e_2 = keep.tile([P, PACK * widest], F32, name="e_2", tag="w1_codes" if c % 2 else "free", align_bytes=64)
            elif E2MODE == 5:
                e_2 = keep.tile([P, PACK * widest], F32, name="e_2", tag="w1_codes" if c % 2 else "stage0", align_bytes=64)
            else:
                e_2 = ring.tile([P, PACK * widest], F32, name="e_2", bufs=E2MODE)
            for t in range(PACK):
                e_1 = ring.tile([P, widest], F32, name="e_1", bufs=E1B)
                nc.scalar.activation(e_1[:, :n], ye[t][:].indirect(sk1_t[:, cols]), ACT.Copy)
                nc.vector.tensor_tensor(mas[:, t * n : (t + 1) * n], y[t][:].indirect(ex_t[:, cols]), e_1[:, :n], ALU.mult)
            for t in range(PACK):
                if c * PACK + t < V2 or (c == len(CHUNKS) - 1 and t >= PACK - V2L):
                    nc.vector.tensor_copy(e_2[:, t * n : (t + 1) * n], ye[t][:].indirect(sk2_t[:, cols]))
                else:
                    nc.scalar.activation(e_2[:, t * n : (t + 1) * n], ye[t][:].indirect(sk2_t[:, cols]), ACT.Copy)
            hid = ring.tile([P, widest, PACK], BF16, name="hid", align_bytes=64)
            nc.vector.tensor_tensor(woven(hid, n), by_rows(mas, n), by_rows(e_2, n), ALU.min)
            codes = ring.tile([P, widest], U32, name="hid_codes", align_bytes=64)
            scales = ring.tile([P, widest], U8, name="hid_scales", align_bytes=64)
            nc.vector.quantize_mx(
                out=codes[:, :n].bitcast(FP8X4), scales=scales[:, :n], in_=hid[:, :n, :].rearrange("p c t -> p (c t)")
            )
            if not w3_box:
                make_w3()
            w3_q = w3_box[0]
            fill = PACK * n // 2 if (SPLIT and c == len(CHUNKS) - 1) else min(BANK, PACK * n)
            banks = [psum.tile([P, BANK], F32, name="bank") for b in range(PACK * n // fill)]
            for t in range(PACK):
                lo = 0
                while lo < n:
                    b, at = divmod(t * n + lo, fill)
                    width = 512 if n == 512 else 256 if min(n - lo, fill - at) >= 256 else min(n, 128)
                    product(banks[b][:, at : at + width], w3_q, t, codes[:, lo : lo + width], scales[:, lo : lo + width])
                    lo = lo + width
            return banks

        def hand_out(r0, n, banks):
            res = ring.tile([P, PACK * widest], F32, name="res", bufs=RESB)
            for b, bank in enumerate(banks):
                used = PACK * n // len(banks)
                if SPLIT == 2 and r0 + n == U and b == 1:
                    nc.vector.tensor_copy(res[:, b * used : (b + 1) * used], bank[:, :used])
                else:
                    nc.scalar.copy(res[:, b * used : (b + 1) * used], bank[:, :used])
            nc.sync.dma_start(out_rows[:, :, r0 : r0 + n], res[:, : PACK * n].rearrange("p (t c) -> p t c", t=PACK))
            rounded = ring.tile([P, widest, PACK], BF16, name="rounded", align_bytes=64)
            nc.vector.tensor_copy(woven(rounded, n), by_rows(res, n))
            nc.vector.quantize_mx(
                out=out_codes[:, r0 : r0 + n].bitcast(FP8X4),
                scales=out_scales[:, r0 : r0 + n],
                in_=rounded[:, :n, :].rearrange("p c t -> p (c t)"),
            )
            nc.sync.dma_start(out_words[:, r0 : r0 + n], out_codes[:, r0 : r0 + n].bitcast(I32))

        pending = None
        r0 = 0
        for c, n in enumerate(CHUNKS):
            banks = hidden(c, r0, n)
            if pending is not None:
                hand_out(*pending)
            pending = (r0, n, banks)
            r0 = r0 + n
        hand_out(*pending)
        for q in range(4):
            queue = nc.scalar if q % 2 else nc.sync
            queue.dma_start(out_2[0, 4 * q : 4 * q + 4, :].bitcast(I32), out_scales[32 * q : 32 * q + 4, :].bitcast(I32))
